import numpy as np
import ml_dtypes


def mxq(x, axis, fmt="e4m3"):
    dtype, down = {"e4m3": (ml_dtypes.float8_e4m3fn, 7), "e5m2": (ml_dtypes.float8_e5m2, 14)}[fmt]
    v = np.moveaxis(np.asarray(x, np.float32).astype(ml_dtypes.bfloat16).astype(np.float64), axis, -1)
    blocks = v.reshape(v.shape[:-1] + (-1, 32))
    amax = np.abs(blocks).max(-1, keepdims=True)
    byte = np.maximum(np.where(amax > 0, np.frexp(amax)[1] - 1 + 127, 0) - down, 1)
    scale = np.exp2(byte - 127.0)
    codes = (blocks / scale).astype(np.float32).astype(dtype).astype(np.float64)
    return np.moveaxis((codes * scale).reshape(v.shape), -1, axis)


WIDE = False


def mx_kscale(k):
    if not WIDE:
        return np.ones(k)
    levels = np.array([10, -10, 5, -5, 0])
    if k % 512:
        return np.exp2(np.random.permutation(np.resize(levels, k // 32))).repeat(32)
    a = np.empty((k // 512, 16))
    for p in range(k // 512):
        a[p, :8] = np.random.permutation(np.resize(levels, 8))
        for g in range(8):
            far = levels[np.abs(levels - a[p, g]) >= 10]
            a[p, g + 8] = far[np.random.randint(len(far))]
    return np.exp2(a.ravel()).repeat(32)


BF16 = ml_dtypes.bfloat16


def bf(x):
    return np.asarray(x, np.float32).astype(BF16)


def f64(x):
    return np.asarray(x).astype(np.float64)


E2M1 = np.array([0.0, 0.5, 1.0, 1.5, 2.0, 3.0, 4.0, 6.0, -0.0, -0.5, -1.0, -1.5, -2.0, -3.0, -4.0, -6.0])


def pack_weight(w, fmt):
    k, n = w.shape
    w = f64(bf(w)).reshape(k // 32, 32, n)
    amax = np.abs(w).max(1)
    if fmt == "e4m3":
        byte = np.frexp(amax)[1] - 1 + 127 - 7
    else:
        mant, ex = np.frexp(amax / 6.0)
        byte = np.where(mant > 0.5, ex, ex - 1) + 127
    byte = np.clip(np.where(amax > 0, byte, 1), 1, 254)
    scaled = (w * np.exp2(127.0 - byte)[:, None, :]).reshape(k, n).astype(np.float32)
    by_word = np.ascontiguousarray(scaled.reshape(k // 512, 128, 4, n).transpose(0, 1, 3, 2))
    if fmt == "e4m3":
        words = by_word.astype(ml_dtypes.float8_e4m3fn).view(np.uint8)
    else:
        c = by_word.astype(ml_dtypes.float4_e2m1fn).view(np.uint8) & 0xF
        words = c[..., 0::2] | (c[..., 1::2] << 4)
    return np.ascontiguousarray(words), np.ascontiguousarray(byte.astype(np.uint8).reshape(k // 512, 16, n))


def unpack_weight(words, scales, fmt):
    g, p, n, _ = words.shape
    if fmt == "e4m3":
        vals = np.ascontiguousarray(words).view(ml_dtypes.float8_e4m3fn).astype(np.float64)
    else:
        nib = np.empty((g, p, n, 4), np.uint8)
        nib[..., 0::2] = words & 0xF
        nib[..., 1::2] = words >> 4
        vals = E2M1[nib]
    vals = vals * np.repeat(np.exp2(scales.astype(np.float64) - 127.0), 8, axis=1)[..., None]
    return vals.transpose(0, 1, 3, 2).reshape(g * 512, n)
def pack4(w):
    words, scales = pack_weight(w, "e2m1")
    return words.reshape(words.shape[0], 128, -1), scales


def unpack4(words, scales):
    return unpack_weight(words.reshape(words.shape[0], 128, -1, 2), scales, "e2m1")


B, T, G, L, C = 4, 1024, 2, 512, 512

WET = 0.33


def setup_inputs():
    s, u, v = mx_kscale(T), mx_kscale(C), mx_kscale(T)
    x = bf(np.random.standard_normal((B, T, C)) * s[:, None] * u)
    swing_words, swing_scales = pack4(WET * np.random.standard_normal((T, T)) / np.sqrt(T) / s[:, None] * v)
    bleed_words, bleed_scales = pack4(WET * np.random.standard_normal((C, C)) / np.sqrt(C) / u[:, None])
    accent_words, accent_scales = pack4(WET * np.random.standard_normal((T, L)) / np.sqrt(L) / v[:, None])
    return {"x": x,
            "swing_words": swing_words, "swing_scales": swing_scales,
            "step_dry": bf((1 + 0.1 * np.random.standard_normal(T)) * v / s),
            "bleed_words": bleed_words, "bleed_scales": bleed_scales,
            "channel_dry": bf((1 + 0.1 * np.random.standard_normal(C)) / u),
            "accent_words": accent_words, "accent_scales": accent_scales,
            "accent_dry": bf((1 + 0.1 * np.random.standard_normal(T)) / v)}


def reference(x, swing_words, swing_scales, step_dry, bleed_words, bleed_scales, channel_dry, accent_words, accent_scales, accent_dry):
    swing = unpack4(swing_words, swing_scales)
    bleed = unpack4(bleed_words, bleed_scales)
    accent = unpack4(accent_words, accent_scales).reshape(G, L, L)
    x = f64(x)
    y = x * f64(step_dry)[:, None] + (swing.T @ mxq(x, 1, "e4m3"))
    z = y * f64(channel_dry) + (mxq(y, 2, "e4m3") @ bleed)
    z = z.reshape(B, G, L, C)
    out = z * f64(accent_dry).reshape(G, L, 1) + (accent.swapaxes(1, 2) @ mxq(z, 2, "e4m3"))
    return out.reshape(B, T, C)

@@ -1,0 +1,277 @@
+from contextlib import ExitStack
+
+import concourse.mybir as mybir
+from concourse.masks import make_identity
+
+B, T, C = 4, 1024, 512
+FLOPS = 2 * (B * T * T * C + B * T * C * C + B * T * 512 * C)
+
+F32 = mybir.dt.float32
+BF16 = mybir.dt.bfloat16
+I32 = mybir.dt.int32
+U32 = mybir.dt.uint32
+U8 = mybir.dt.uint8
+FP8X4 = mybir.dt.float8_e4m3fn_x4
+FP4X4 = mybir.dt.float4_e2m1fn_x4
+ADD = mybir.AluOpType.add
+MULT = mybir.AluOpType.mult
+
+UNITS = 8
+HEAD_V = 224
+STEADY_V = 64
+OFF = {0: (3,), 1: (3,), 2: (3,), 3: (3,), 4: (3,), 5: (3,), 6: (3,), 7: (3,)}
+
+
+def tile_drum_loop_corrections_t2_kernel(tc, x, swing_words, swing_scales, step_dry, bleed_words, bleed_scales, channel_dry, accent_words, accent_scales, accent_dry, out):
+    nc = tc.nc
+    with ExitStack() as ctx:
+        keep = ctx.enter_context(tc.tile_pool(name="keep", bufs=1))
+        work = ctx.enter_context(tc.tile_pool(name="work", bufs=2))
+        psum = ctx.enter_context(tc.psum_pool(name="psum", bufs=2))
+
+        ident = keep.tile([128, 128], F32, name="ident")
+        xs = [keep.tile([128, 4, C], BF16, name="x%d" % i, align_bytes=256) for i in range(UNITS)]
+        sw_raw = [keep.tile([128, 2, 1024], U8, name="sw_raw%d" % h, align_bytes=256) for h in range(2)]
+        sw = [keep.tile([128, 2, 4, 256], U8, name="sw%d" % h, align_bytes=256) for h in range(2)]
+        sws_raw = keep.tile([128, 2, 1024], U8, name="sws_raw", align_bytes=256)
+        sws = [keep.tile([128, 2, 4, 128], U8, name="sws%d" % h, align_bytes=256) for h in range(2)]
+        ac_raw = keep.tile([128, 2, 1024], U8, name="ac_raw", align_bytes=256)
+        ac = [keep.tile([128, 4, 256], U8, name="ac%d" % h, align_bytes=256) for h in range(2)]
+        acs_raw = keep.tile([128, 2, 512], U8, name="acs_raw", align_bytes=256)
+        acs = [keep.tile([128, 4, 128], U8, name="acs%d" % h, align_bytes=256) for h in range(2)]
+        bl = keep.tile([128, 1024], U8, name="bl", align_bytes=256)
+        bls = keep.tile([128, 512], U8, name="bls", align_bytes=256)
+        sd = keep.tile([128, 2, 4], BF16, name="sd")
+        ad = keep.tile([128, 2, 4], BF16, name="ad")
+        cd = keep.tile([128, C], BF16, name="cd")
+
+        ctx.enter_context(tc.manual_schedule())
+
+        nc.vector.memset(sws_raw[:].bitcast(I32), 0)
+        nc.gpsimd.memset(bls[:].bitcast(I32), 0)
+        nc.gpsimd.memset(acs_raw[:].bitcast(I32), 0)
+        make_identity(nc, ident[:])
+
+        def load_x(i):
+            b, g = divmod(i, 2)
+            nc.sync.dma_start(out=xs[i][:], in_=x[b, 512 * g : 512 * g + 512, :].rearrange("(p t) c -> p t c", t=4))
+
+        def load_swing(h):
+            nc.sync.dma_start(out=sw_raw[h][:].bitcast(I32), in_=swing_words.bitcast(I32)[:, :, 256 * h : 256 * h + 256].rearrange("g p n -> p g n"))
+
+        def load_scales(dst, src):
+            for q in range(4):
+                nc.sync.dma_start(out=dst[32 * q : 32 * q + 4, :, :].bitcast(I32), in_=src.bitcast(I32)[:, 4 * q : 4 * q + 4, :].rearrange("g r n -> r g n"))
+
+        load_x(0)
+        load_swing(0)
+        load_scales(sws_raw, swing_scales)
+        load_x(1)
+        nc.sync.dma_start(out=sd[:], in_=step_dry.rearrange("(h m t) -> m h t", h=2, t=4))
+        load_x(2)
+        nc.sync.dma_start(out=bl[:].bitcast(I32), in_=bleed_words.bitcast(I32)[0])
+        nc.sync.dma_start(out=cd[:], in_=channel_dry.partition_broadcast(128))
+        for q in range(4):
+            nc.sync.dma_start(out=bls[32 * q : 32 * q + 4, :].bitcast(I32), in_=bleed_scales.bitcast(I32)[0, 4 * q : 4 * q + 4, :])
+        load_swing(1)
+        load_x(3)
+        nc.sync.dma_start(out=ac_raw[:].bitcast(I32), in_=accent_words.bitcast(I32).rearrange("g p n -> p g n"))
+        load_scales(acs_raw, accent_scales)
+        nc.sync.dma_start(out=ad[:], in_=accent_dry.rearrange("(h m t) -> m h t", h=2, t=4))
+        for i in range(4, UNITS):
+            load_x(i)
+
+        xg = {}
+        xq = {}
+        ybf = {}
+        yq = {}
+        y = {}
+        ycd = {}
+        z = {}
+        zbf = {}
+        zq = {}
+        o = {}
+        pa = {}
+        pc = {}
+        ext = {}
+
+        def interleave(copy, i, c0, c1):
+            if i not in xg:
+                xg[i] = work.tile([128, C, 4], BF16, name="xg", align_bytes=256, bufs=3)
+            copy(
+                out=xg[i][:, c0:c1, :].rearrange("p (c i) t -> p c t i", i=4),
+                in_=xs[i][:, :, c0:c1].rearrange("p t (c i) -> p c t i", i=4),
+            )
+
+        def quantize(src, name, bufs):
+            codes = work.tile([128, 512], U32, name=name, align_bytes=256, bufs=bufs)
+            scales = work.tile([128, 512], U8, name=name + "s", align_bytes=256, bufs=bufs)
+            nc.vector.quantize_mx(out=codes[:].bitcast(FP8X4), scales=scales[:], in_=src[:].rearrange("p n t -> p (n t)"))
+            return codes, scales
+
+        def quant_x(i):
+            xq[i] = quantize(xg[i], "xq", 6)
+
+        def perm_swing(h):
+            for g in range(2):
+                nc.vector.tensor_copy(out=sw[h][:, g, :, :].rearrange("p t (m e) -> p t m e", e=2), in_=sw_raw[h][:, g, :].rearrange("p (m t e) -> p t m e", t=4, e=2))
+
+        def perm_swing_scales(h):
+            nc.vector.tensor_copy(out=sws[h][:], in_=sws_raw[:, :, 512 * h : 512 * h + 512].rearrange("p g (m t) -> p g t m", t=4))
+
+        def perm_accent(h):
+            nc.vector.tensor_copy(out=ac[h][:].rearrange("p t (m e) -> p t m e", e=2), in_=ac_raw[:, h, :].rearrange("p (m t e) -> p t m e", t=4, e=2))
+            nc.vector.tensor_copy(out=acs[h][:], in_=acs_raw[:, h, :].rearrange("p (m t) -> p t m", t=4))
+
+        def s1_pass(u, k):
+            b, h = divmod(u, 2)
+            t, g = divmod(k, 2)
+            if g == 0:
+                pa[u, t] = psum.tile([128, 512], F32, name="pa", bufs=4)
+            codes, scales = xq[2 * b + g]
+            nc.tensor.matmul_mx(out=pa[u, t][:], lhsT=sw[h][:, g, t, :].bitcast(FP4X4), lhsT_scale=sws[h][:, g, t, :], rhs=codes[:].bitcast(FP8X4), rhs_scale=scales[:], start=(g == 0), stop=(g == 1))
+
+        def c_add(u, t):
+            h = u % 2
+            if t == 0:
+                y[u] = work.tile([128, 4, C], F32, name="y")
+            nc.vector.scalar_tensor_tensor(out=y[u][:, t, :].rearrange("p (q w) -> p q w", q=4), in0=xs[u][:, t, :].rearrange("p (w q) -> p q w", q=4), scalar=sd[:, h, t : t + 1], in1=pa[u, t][:].rearrange("p (w q) -> p q w", q=4), op0=MULT, op1=ADD)
+
+        def turn(u, t):
+            pb = psum.tile([128, 4, 128], F32, name="pb", bufs=2)
+            for q in range(4):
+                nc.tensor.transpose(pb[:, q, :], y[u][:, t, 128 * q : 128 * q + 128], ident[:])
+            if t == 0:
+                ybf[u] = work.tile([128, 512, 4], BF16, name="ybf", align_bytes=256)
+            nc.scalar.copy(out=ybf[u][:, 128 * t : 128 * t + 128, :], in_=pb[:].rearrange("p q m -> p m q"))
+
+        def f_mul(u, t):
+            if t == 0:
+                ycd[u] = work.tile([128, 4, C], F32, name="ycd")
+            nc.gpsimd.tensor_tensor(out=ycd[u][:, t, :].rearrange("p (w q) -> p w q", q=4), in0=y[u][:, t, :].rearrange("p (q w) -> p w q", q=4), in1=cd[:].rearrange("p (w q) -> p w q", q=4), op=MULT)
+
+        def quant_y(u):
+            yq[u] = quantize(ybf[u], "yq", 2)
+
+        def s2(u, t):
+            pc[2, u, t] = psum.tile([128, 512], F32, name="pc", bufs=2)
+            codes, scales = yq[u]
+            nc.tensor.matmul_mx(out=pc[2, u, t][:], lhsT=codes[:, 128 * t : 128 * t + 128].bitcast(FP8X4), lhsT_scale=scales[:, 128 * t : 128 * t + 128], rhs=bl[:].bitcast(FP4X4), rhs_scale=bls[:], start=True, stop=True)
+
+        def z_tile(u):
+            if u not in z:
+                z[u] = work.tile([128, 4, C], F32, name="z", bufs=3)
+            return z[u]
+
+        def g_add(u, t):
+            nc.vector.tensor_tensor(out=z_tile(u)[:, t, :], in0=pc[2, u, t][:], in1=ycd[u][:, t, :], op=ADD)
+
+        def g_off(u, t):
+            ext[u, t] = work.tile([128, C], F32, name="ext")
+            nc.scalar.copy(out=ext[u, t][:], in_=pc[2, u, t][:])
+            nc.gpsimd.tensor_tensor(out=z_tile(u)[:, t, :], in0=ext[u, t][:], in1=ycd[u][:, t, :], op=ADD)
+
+        def h_round(copy, u, c0, c1):
+            if u not in zbf:
+                zbf[u] = work.tile([128, C, 4], BF16, name="zbf", align_bytes=256)
+            copy(out=zbf[u][:, c0:c1, :].rearrange("p (c i) t -> p c t i", i=4), in_=z[u][:, :, c0:c1].rearrange("p t (c i) -> p c t i", i=4))
+
+        def quant_z(u):
+            zq[u] = quantize(zbf[u], "zq", 2)
+
+        def s3(u, t):
+            h = u % 2
+            pc[3, u, t] = psum.tile([128, 512], F32, name="pc", bufs=2)
+            codes, scales = zq[u]
+            nc.tensor.matmul_mx(out=pc[3, u, t][:], lhsT=ac[h][:, t, :].bitcast(FP4X4), lhsT_scale=acs[h][:, t, :], rhs=codes[:].bitcast(FP8X4), rhs_scale=scales[:], start=True, stop=True)
+
+        def j_add(u, t):
+            b, h = divmod(u, 2)
+            if t == 0:
+                o[u] = work.tile([128, 4, C], F32, name="o")
+            nc.vector.scalar_tensor_tensor(out=o[u][:, t, :], in0=z[u][:, t, :], scalar=ad[:, h, t : t + 1], in1=pc[3, u, t][:], op0=MULT, op1=ADD)
+            rows = out[b, 512 * h : 512 * h + 512, :].rearrange("(p t) c -> p t c", t=4)
+            if u == UNITS - 1:
+                nc.sync.dma_start(out=rows[:, t, :], in_=o[u][:, t, :])
+            elif t == 3:
+                nc.sync.dma_start(out=rows, in_=o[u][:])
+
+        interleave(nc.scalar.copy, 0, HEAD_V, C)
+        interleave(nc.vector.tensor_copy, 0, 0, HEAD_V)
+        interleave(nc.scalar.copy, 1, HEAD_V, C)
+        perm_swing(0)
+        interleave(nc.vector.tensor_copy, 1, 0, HEAD_V)
+        quant_x(0)
+        perm_swing_scales(0)
+        quant_x(1)
+        for k in range(8):
+            s1_pass(0, k)
+        interleave(nc.scalar.copy, 2, 0, C)
+
+        for s in range(UNITS + 2):
+            off = OFF[s - 1] if 0 <= s - 1 < UNITS else ()
+            fills = []
+            users = []
+            if 0 <= s - 1 < UNITS:
+                order = [t for t in range(4) if t not in off]
+                fills += [(2, s - 1, t) for t in list(off) + order]
+                users += [(g_add, s - 1, t) for t in order]
+            if 0 <= s - 2 < UNITS:
+                fills += [(3, s - 2, t) for t in range(4)]
+                users += [(j_add, s - 2, t) for t in range(4)]
+            done_fills = 0
+
+            def fill():
+                stage, u, t = fills.pop(0)
+                if stage == 2:
+                    s2(u, t)
+                else:
+                    s3(u, t)
+
+            for k in range(min(2, len(fills))):
+                fill()
+            for t in off:
+                g_off(s - 1, t)
+                if fills:
+                    fill()
+            if s < UNITS:
+                for t in range(4):
+                    c_add(s, t)
+                    turn(s, t)
+                    f_mul(s, t)
+            if s == 0:
+                perm_swing(1)
+                perm_swing_scales(1)
+            passes = list(range(8)) if s + 1 < UNITS else []
+            ai = s + 3
+            halves = 2 if ai < UNITS else 0
+            if halves:
+                mid = (STEADY_V + C) // 2
+                interleave(nc.scalar.copy, ai, STEADY_V, mid)
+            n_g = len([1 for e in users if e[1] == s - 1])
+            for k, (fn, u, t) in enumerate(users):
+                fn(u, t)
+                if fills:
+                    fill()
+                if passes:
+                    s1_pass(s + 1, passes.pop(0))
+                if k == n_g - 1:
+                    h_round(nc.scalar.copy, s - 1, 0, 256)
+                    h_round(nc.scalar.copy, s - 1, 256, 512)
+            while passes:
+                s1_pass(s + 1, passes.pop(0))
+            if halves:
+                interleave(nc.scalar.copy, ai, mid, C)
+                interleave(nc.vector.tensor_copy, ai, 0, STEADY_V)
+            if s == 0:
+                perm_accent(0)
+            if s == 1:
+                perm_accent(1)
+            if s == 0:
+                quant_x(2)
+            if s < UNITS:
+                quant_y(s)
+            if halves:
+                quant_x(ai)
+            if 0 <= s - 1 < UNITS:
+                quant_z(s - 1)

@@ -17,8 +17,7 @@ ADD = mybir.AluOpType.add
 MULT = mybir.AluOpType.mult
 
 UNITS = 8
-HEAD_V = 224
-STEADY_V = 64
+HEAD_V = 128
 OFF = {0: (3,), 1: (3,), 2: (3,), 3: (3,), 4: (3,), 5: (3,), 6: (3,), 7: (3,)}
 
 
@@ -63,9 +62,10 @@ def tile_drum_loop_corrections_t2_kernel(tc, x, swing_words, swing_scales, step_
             for q in range(4):
                 nc.sync.dma_start(out=dst[32 * q : 32 * q + 4, :, :].bitcast(I32), in_=src.bitcast(I32)[:, 4 * q : 4 * q + 4, :].rearrange("g r n -> r g n"))
 
-        load_x(0)
         load_swing(0)
         load_scales(sws_raw, swing_scales)
+        load_x(0)
+        load_swing(1)
         load_x(1)
         nc.sync.dma_start(out=sd[:], in_=step_dry.rearrange("(h m t) -> m h t", h=2, t=4))
         load_x(2)
@@ -73,7 +73,6 @@ def tile_drum_loop_corrections_t2_kernel(tc, x, swing_words, swing_scales, step_
         nc.sync.dma_start(out=cd[:], in_=channel_dry.partition_broadcast(128))
         for q in range(4):
             nc.sync.dma_start(out=bls[32 * q : 32 * q + 4, :].bitcast(I32), in_=bleed_scales.bitcast(I32)[0, 4 * q : 4 * q + 4, :])
-        load_swing(1)
         load_x(3)
         nc.sync.dma_start(out=ac_raw[:].bitcast(I32), in_=accent_words.bitcast(I32).rearrange("g p n -> p g n"))
         load_scales(acs_raw, accent_scales)
@@ -135,12 +134,12 @@ def tile_drum_loop_corrections_t2_kernel(tc, x, swing_words, swing_scales, step_
             h = u % 2
             if t == 0:
                 y[u] = work.tile([128, 4, C], F32, name="y")
-            nc.vector.scalar_tensor_tensor(out=y[u][:, t, :].rearrange("p (q w) -> p q w", q=4), in0=xs[u][:, t, :].rearrange("p (w q) -> p q w", q=4), scalar=sd[:, h, t : t + 1], in1=pa[u, t][:].rearrange("p (w q) -> p q w", q=4), op0=MULT, op1=ADD)
+            nc.vector.scalar_tensor_tensor(out=y[u][:, t, :], in0=xs[u][:, t, :], scalar=sd[:, h, t : t + 1], in1=pa[u, t][:], op0=MULT, op1=ADD)
 
         def turn(u, t):
             pb = psum.tile([128, 4, 128], F32, name="pb", bufs=2)
             for q in range(4):
-                nc.tensor.transpose(pb[:, q, :], y[u][:, t, 128 * q : 128 * q + 128], ident[:])
+                nc.tensor.transpose(pb[:, q, :], y[u][:, t, q:C:4], ident[:])
             if t == 0:
                 ybf[u] = work.tile([128, 512, 4], BF16, name="ybf", align_bytes=256)
             nc.scalar.copy(out=ybf[u][:, 128 * t : 128 * t + 128, :], in_=pb[:].rearrange("p q m -> p m q"))
@@ -148,7 +147,7 @@ def tile_drum_loop_corrections_t2_kernel(tc, x, swing_words, swing_scales, step_
         def f_mul(u, t):
             if t == 0:
                 ycd[u] = work.tile([128, 4, C], F32, name="ycd")
-            nc.gpsimd.tensor_tensor(out=ycd[u][:, t, :].rearrange("p (w q) -> p w q", q=4), in0=y[u][:, t, :].rearrange("p (q w) -> p w q", q=4), in1=cd[:].rearrange("p (w q) -> p w q", q=4), op=MULT)
+            nc.gpsimd.tensor_tensor(out=ycd[u][:, t, :], in0=y[u][:, t, :], in1=cd[:], op=MULT)
 
         def quant_y(u):
             yq[u] = quantize(ybf[u], "yq", 2)
@@ -197,12 +196,14 @@ def tile_drum_loop_corrections_t2_kernel(tc, x, swing_words, swing_scales, step_
                 nc.sync.dma_start(out=rows, in_=o[u][:])
 
         interleave(nc.scalar.copy, 0, HEAD_V, C)
-        interleave(nc.vector.tensor_copy, 0, 0, HEAD_V)
         interleave(nc.scalar.copy, 1, HEAD_V, C)
         perm_swing(0)
+        interleave(nc.vector.tensor_copy, 0, 0, HEAD_V)
+        perm_swing(1)
         interleave(nc.vector.tensor_copy, 1, 0, HEAD_V)
-        quant_x(0)
         perm_swing_scales(0)
+        quant_x(0)
+        perm_swing_scales(1)
         quant_x(1)
         for k in range(8):
             s1_pass(0, k)
@@ -219,7 +220,6 @@ def tile_drum_loop_corrections_t2_kernel(tc, x, swing_words, swing_scales, step_
             if 0 <= s - 2 < UNITS:
                 fills += [(3, s - 2, t) for t in range(4)]
                 users += [(j_add, s - 2, t) for t in range(4)]
-            done_fills = 0
 
             def fill():
                 stage, u, t = fills.pop(0)
@@ -234,20 +234,17 @@ def tile_drum_loop_corrections_t2_kernel(tc, x, swing_words, swing_scales, step_
                 g_off(s - 1, t)
                 if fills:
                     fill()
+            ai = s + 3
+            if ai < UNITS:
+                interleave(nc.scalar.copy, ai, 0, 256)
             if s < UNITS:
                 for t in range(4):
                     c_add(s, t)
                     turn(s, t)
                     f_mul(s, t)
-            if s == 0:
-                perm_swing(1)
-                perm_swing_scales(1)
             passes = list(range(8)) if s + 1 < UNITS else []
-            ai = s + 3
-            halves = 2 if ai < UNITS else 0
-            if halves:
-                mid = (STEADY_V + C) // 2
-                interleave(nc.scalar.copy, ai, STEADY_V, mid)
+            if ai < UNITS:
+                interleave(nc.scalar.copy, ai, 256, C)
             n_g = len([1 for e in users if e[1] == s - 1])
             for k, (fn, u, t) in enumerate(users):
                 fn(u, t)
@@ -260,9 +257,6 @@ def tile_drum_loop_corrections_t2_kernel(tc, x, swing_words, swing_scales, step_
                     h_round(nc.scalar.copy, s - 1, 256, 512)
             while passes:
                 s1_pass(s + 1, passes.pop(0))
-            if halves:
-                interleave(nc.scalar.copy, ai, mid, C)
-                interleave(nc.vector.tensor_copy, ai, 0, STEADY_V)
             if s == 0:
                 perm_accent(0)
             if s == 1:
@@ -271,7 +265,7 @@ def tile_drum_loop_corrections_t2_kernel(tc, x, swing_words, swing_scales, step_
                 quant_x(2)
             if s < UNITS:
                 quant_y(s)
-            if halves:
+            if ai < UNITS:
                 quant_x(ai)
             if 0 <= s - 1 < UNITS:
                 quant_z(s - 1)

@@ -17,8 +17,8 @@ ADD = mybir.AluOpType.add
 MULT = mybir.AluOpType.mult
 
 UNITS = 8
-HEAD_V = 128
-OFF = {0: (3,), 1: (3,), 2: (3,), 3: (3,), 4: (3,), 5: (3,), 6: (3,), 7: (3,)}
+HEAD_V = 192
+OFF = {0: (), 1: (3,), 2: (3,), 3: (3,), 4: (3,), 5: (3,), 6: (3,), 7: (3,)}
 
 
 def tile_drum_loop_corrections_t2_kernel(tc, x, swing_words, swing_scales, step_dry, bleed_words, bleed_scales, channel_dry, accent_words, accent_scales, accent_dry, out):
@@ -126,7 +126,7 @@ def tile_drum_loop_corrections_t2_kernel(tc, x, swing_words, swing_scales, step_
             b, h = divmod(u, 2)
             t, g = divmod(k, 2)
             if g == 0:
-                pa[u, t] = psum.tile([128, 512], F32, name="pa", bufs=4)
+                pa[u, t] = psum.tile([128, 512], F32, name="pa", bufs=3)
             codes, scales = xq[2 * b + g]
             nc.tensor.matmul_mx(out=pa[u, t][:], lhsT=sw[h][:, g, t, :].bitcast(FP4X4), lhsT_scale=sws[h][:, g, t, :], rhs=codes[:].bitcast(FP8X4), rhs_scale=scales[:], start=(g == 0), stop=(g == 1))
 
@@ -144,16 +144,16 @@ def tile_drum_loop_corrections_t2_kernel(tc, x, swing_words, swing_scales, step_
                 ybf[u] = work.tile([128, 512, 4], BF16, name="ybf", align_bytes=256)
             nc.scalar.copy(out=ybf[u][:, 128 * t : 128 * t + 128, :], in_=pb[:].rearrange("p q m -> p m q"))
 
-        def f_mul(u, t):
+        def f_mul(engine, u, t):
             if t == 0:
                 ycd[u] = work.tile([128, 4, C], F32, name="ycd")
-            nc.gpsimd.tensor_tensor(out=ycd[u][:, t, :], in0=y[u][:, t, :], in1=cd[:], op=MULT)
+            engine.tensor_tensor(out=ycd[u][:, t, :], in0=y[u][:, t, :], in1=cd[:], op=MULT)
 
         def quant_y(u):
             yq[u] = quantize(ybf[u], "yq", 2)
 
         def s2(u, t):
-            pc[2, u, t] = psum.tile([128, 512], F32, name="pc", bufs=2)
+            pc[2, u, t] = psum.tile([128, 512], F32, name="pc", bufs=3)
             codes, scales = yq[u]
             nc.tensor.matmul_mx(out=pc[2, u, t][:], lhsT=codes[:, 128 * t : 128 * t + 128].bitcast(FP8X4), lhsT_scale=scales[:, 128 * t : 128 * t + 128], rhs=bl[:].bitcast(FP4X4), rhs_scale=bls[:], start=True, stop=True)
 
@@ -180,7 +180,7 @@ def tile_drum_loop_corrections_t2_kernel(tc, x, swing_words, swing_scales, step_
 
         def s3(u, t):
             h = u % 2
-            pc[3, u, t] = psum.tile([128, 512], F32, name="pc", bufs=2)
+            pc[3, u, t] = psum.tile([128, 512], F32, name="pc", bufs=3)
             codes, scales = zq[u]
             nc.tensor.matmul_mx(out=pc[3, u, t][:], lhsT=ac[h][:, t, :].bitcast(FP4X4), lhsT_scale=acs[h][:, t, :], rhs=codes[:].bitcast(FP8X4), rhs_scale=scales[:], start=True, stop=True)
 
@@ -199,73 +199,99 @@ def tile_drum_loop_corrections_t2_kernel(tc, x, swing_words, swing_scales, step_
         interleave(nc.scalar.copy, 1, HEAD_V, C)
         perm_swing(0)
         interleave(nc.vector.tensor_copy, 0, 0, HEAD_V)
-        perm_swing(1)
-        interleave(nc.vector.tensor_copy, 1, 0, HEAD_V)
         perm_swing_scales(0)
         quant_x(0)
-        perm_swing_scales(1)
+        perm_swing(1)
+        interleave(nc.vector.tensor_copy, 1, 0, HEAD_V)
         quant_x(1)
-        for k in range(8):
+        for k in (0, 2, 4, 1, 3, 5):
             s1_pass(0, k)
         interleave(nc.scalar.copy, 2, 0, C)
 
         for s in range(UNITS + 2):
-            off = OFF[s - 1] if 0 <= s - 1 < UNITS else ()
-            fills = []
-            users = []
-            if 0 <= s - 1 < UNITS:
-                order = [t for t in range(4) if t not in off]
-                fills += [(2, s - 1, t) for t in list(off) + order]
-                users += [(g_add, s - 1, t) for t in order]
-            if 0 <= s - 2 < UNITS:
-                fills += [(3, s - 2, t) for t in range(4)]
-                users += [(j_add, s - 2, t) for t in range(4)]
+            z_unit = s - 1 if 0 <= s - 1 < UNITS else None
+            o_unit = s - 2 if 0 <= s - 2 < UNITS else None
+            off = OFF[z_unit] if z_unit is not None else ()
+            own = [t for t in range(4) if t not in off] if z_unit is not None else []
+            fills = [(s2, z_unit, t) for t in list(off) + own]
+            if o_unit is not None:
+                fills += [(s3, o_unit, t) for t in range(4)]
 
             def fill():
-                stage, u, t = fills.pop(0)
-                if stage == 2:
-                    s2(u, t)
-                else:
-                    s3(u, t)
-
-            for k in range(min(2, len(fills))):
-                fill()
-            for t in off:
-                g_off(s - 1, t)
                 if fills:
-                    fill()
+                    fn, u, t = fills.pop(0)
+                    fn(u, t)
+
+            late = [6, 7] if s < UNITS else []
+            early = list(range(6)) if s + 1 < UNITS else []
+
+            def swing_pass():
+                if early:
+                    s1_pass(s + 1, early.pop(0))
+
+            def c_pair(t0):
+                for t in (t0, t0 + 1):
+                    c_add(s, t)
+                    if s > 0 or t < 2:
+                        f_mul(nc.gpsimd, s, t)
+                turn(s, t0)
+                if t0 == 0:
+                    for k in late:
+                        s1_pass(s, k)
+                else:
+                    if s > 0:
+                        swing_pass()
+                        swing_pass()
+                    if o_unit is not None:
+                        j_add(o_unit, 0)
+                        fill()
+                turn(s, t0 + 1)
+
+            fill()
+            fill()
+            fill()
+            for t in off:
+                g_off(z_unit, t)
+                fill()
             ai = s + 3
-            if ai < UNITS:
+            if ai < UNITS and s > 0:
                 interleave(nc.scalar.copy, ai, 0, 256)
             if s < UNITS:
-                for t in range(4):
-                    c_add(s, t)
-                    turn(s, t)
-                    f_mul(s, t)
-            passes = list(range(8)) if s + 1 < UNITS else []
-            if ai < UNITS:
-                interleave(nc.scalar.copy, ai, 256, C)
-            n_g = len([1 for e in users if e[1] == s - 1])
-            for k, (fn, u, t) in enumerate(users):
-                fn(u, t)
-                if fills:
+                c_pair(0)
+            for n, t in enumerate(own):
+                g_add(z_unit, t)
+                fill()
+                if n < 2:
+                    swing_pass()
+            if z_unit is not None:
+                h_round(nc.scalar.copy, z_unit, 0, 256)
+                h_round(nc.scalar.copy, z_unit, 256, 512)
+            if s < UNITS:
+                c_pair(2)
+            if s == 0:
+                perm_swing_scales(1)
+                f_mul(nc.vector, 0, 2)
+                f_mul(nc.vector, 0, 3)
+            if o_unit is not None:
+                for t in range(0 if s >= UNITS else 1, 4):
+                    j_add(o_unit, t)
                     fill()
-                if passes:
-                    s1_pass(s + 1, passes.pop(0))
-                if k == n_g - 1:
-                    h_round(nc.scalar.copy, s - 1, 0, 256)
-                    h_round(nc.scalar.copy, s - 1, 256, 512)
-            while passes:
-                s1_pass(s + 1, passes.pop(0))
+                    swing_pass()
             if s == 0:
-                perm_accent(0)
-            if s == 1:
-                perm_accent(1)
-            if s == 0:
+                interleave(nc.scalar.copy, 3, 0, 256)
+                interleave(nc.vector.tensor_copy, 3, 256, C)
                 quant_x(2)
+            elif ai < UNITS:
+                interleave(nc.scalar.copy, ai, 256, C)
+            while early:
+                swing_pass()
+            if s == 1:
+                perm_accent(0)
+            if s == 2:
+                perm_accent(1)
+            if z_unit is not None:
+                quant_z(z_unit)
             if s < UNITS:
                 quant_y(s)
             if ai < UNITS:
                 quant_x(ai)
-            if 0 <= s - 1 < UNITS:
-                quant_z(s - 1)

from contextlib import ExitStack

import concourse.mybir as mybir
from concourse.masks import make_identity

B, T, C = 4, 1024, 512
FLOPS = 2 * (B * T * T * C + B * T * C * C + B * T * 512 * C)

F32 = mybir.dt.float32
BF16 = mybir.dt.bfloat16
I32 = mybir.dt.int32
U32 = mybir.dt.uint32
U8 = mybir.dt.uint8
FP8X4 = mybir.dt.float8_e4m3fn_x4
FP4X4 = mybir.dt.float4_e2m1fn_x4
ADD = mybir.AluOpType.add
MULT = mybir.AluOpType.mult

UNITS = 8
HEAD_V = 192
OFF = {0: (), 1: (3,), 2: (3,), 3: (3,), 4: (3,), 5: (3,), 6: (3,), 7: (3,)}


def tile_drum_loop_corrections_t2_kernel(tc, x, swing_words, swing_scales, step_dry, bleed_words, bleed_scales, channel_dry, accent_words, accent_scales, accent_dry, out):
    nc = tc.nc
    with ExitStack() as ctx:
        keep = ctx.enter_context(tc.tile_pool(name="keep", bufs=1))
        work = ctx.enter_context(tc.tile_pool(name="work", bufs=2))
        psum = ctx.enter_context(tc.psum_pool(name="psum", bufs=2))

        ident = keep.tile([128, 128], F32, name="ident")
        xs = [keep.tile([128, 4, C], BF16, name="x%d" % i, align_bytes=256) for i in range(UNITS)]
        sw_raw = [keep.tile([128, 2, 1024], U8, name="sw_raw%d" % h, align_bytes=256) for h in range(2)]
        sw = [keep.tile([128, 2, 4, 256], U8, name="sw%d" % h, align_bytes=256) for h in range(2)]
        sws_raw = keep.tile([128, 2, 1024], U8, name="sws_raw", align_bytes=256)
        sws = [keep.tile([128, 2, 4, 128], U8, name="sws%d" % h, align_bytes=256) for h in range(2)]
        ac_raw = keep.tile([128, 2, 1024], U8, name="ac_raw", align_bytes=256)
        ac = [keep.tile([128, 4, 256], U8, name="ac%d" % h, align_bytes=256) for h in range(2)]
        acs_raw = keep.tile([128, 2, 512], U8, name="acs_raw", align_bytes=256)
        acs = [keep.tile([128, 4, 128], U8, name="acs%d" % h, align_bytes=256) for h in range(2)]
        bl = keep.tile([128, 1024], U8, name="bl", align_bytes=256)
        bls = keep.tile([128, 512], U8, name="bls", align_bytes=256)
        sd = keep.tile([128, 2, 4], BF16, name="sd")
        ad = keep.tile([128, 2, 4], BF16, name="ad")
        cd = keep.tile([128, C], BF16, name="cd")

        ctx.enter_context(tc.manual_schedule())

        nc.vector.memset(sws_raw[:].bitcast(I32), 0)
        nc.gpsimd.memset(bls[:].bitcast(I32), 0)
        nc.gpsimd.memset(acs_raw[:].bitcast(I32), 0)
        make_identity(nc, ident[:])

        def load_x(i):
            b, g = divmod(i, 2)
            nc.sync.dma_start(out=xs[i][:], in_=x[b, 512 * g : 512 * g + 512, :].rearrange("(p t) c -> p t c", t=4))

        def load_swing(h):
            nc.sync.dma_start(out=sw_raw[h][:].bitcast(I32), in_=swing_words.bitcast(I32)[:, :, 256 * h : 256 * h + 256].rearrange("g p n -> p g n"))

        def load_scales(dst, src):
            for q in range(4):
                nc.sync.dma_start(out=dst[32 * q : 32 * q + 4, :, :].bitcast(I32), in_=src.bitcast(I32)[:, 4 * q : 4 * q + 4, :].rearrange("g r n -> r g n"))

        load_swing(0)
        load_scales(sws_raw, swing_scales)
        load_x(0)
        load_swing(1)
        load_x(1)
        nc.sync.dma_start(out=sd[:], in_=step_dry.rearrange("(h m t) -> m h t", h=2, t=4))
        load_x(2)
        nc.sync.dma_start(out=bl[:].bitcast(I32), in_=bleed_words.bitcast(I32)[0])
        nc.sync.dma_start(out=cd[:], in_=channel_dry.partition_broadcast(128))
        for q in range(4):
            nc.sync.dma_start(out=bls[32 * q : 32 * q + 4, :].bitcast(I32), in_=bleed_scales.bitcast(I32)[0, 4 * q : 4 * q + 4, :])
        load_x(3)
        nc.sync.dma_start(out=ac_raw[:].bitcast(I32), in_=accent_words.bitcast(I32).rearrange("g p n -> p g n"))
        load_scales(acs_raw, accent_scales)
        nc.sync.dma_start(out=ad[:], in_=accent_dry.rearrange("(h m t) -> m h t", h=2, t=4))
        for i in range(4, UNITS):
            load_x(i)

        xg = {}
        xq = {}
        ybf = {}
        yq = {}
        y = {}
        ycd = {}
        z = {}
        zbf = {}
        zq = {}
        o = {}
        pa = {}
        pc = {}
        ext = {}

        def interleave(copy, i, c0, c1):
            if i not in xg:
                xg[i] = work.tile([128, C, 4], BF16, name="xg", align_bytes=256, bufs=3)
            copy(
                out=xg[i][:, c0:c1, :].rearrange("p (c i) t -> p c t i", i=4),
                in_=xs[i][:, :, c0:c1].rearrange("p t (c i) -> p c t i", i=4),
            )

        def quantize(src, name, bufs):
            codes = work.tile([128, 512], U32, name=name, align_bytes=256, bufs=bufs)
            scales = work.tile([128, 512], U8, name=name + "s", align_bytes=256, bufs=bufs)
            nc.vector.quantize_mx(out=codes[:].bitcast(FP8X4), scales=scales[:], in_=src[:].rearrange("p n t -> p (n t)"))
            return codes, scales

        def quant_x(i):
            xq[i] = quantize(xg[i], "xq", 6)

        def perm_swing(h):
            for g in range(2):
                nc.vector.tensor_copy(out=sw[h][:, g, :, :].rearrange("p t (m e) -> p t m e", e=2), in_=sw_raw[h][:, g, :].rearrange("p (m t e) -> p t m e", t=4, e=2))

        def perm_swing_scales(h):
            nc.vector.tensor_copy(out=sws[h][:], in_=sws_raw[:, :, 512 * h : 512 * h + 512].rearrange("p g (m t) -> p g t m", t=4))

        def perm_accent(h):
            nc.vector.tensor_copy(out=ac[h][:].rearrange("p t (m e) -> p t m e", e=2), in_=ac_raw[:, h, :].rearrange("p (m t e) -> p t m e", t=4, e=2))
            nc.vector.tensor_copy(out=acs[h][:], in_=acs_raw[:, h, :].rearrange("p (m t) -> p t m", t=4))

        def s1_pass(u, k):
            b, h = divmod(u, 2)
            t, g = divmod(k, 2)
            if g == 0:
                pa[u, t] = psum.tile([128, 512], F32, name="pa", bufs=3)
            codes, scales = xq[2 * b + g]
            nc.tensor.matmul_mx(out=pa[u, t][:], lhsT=sw[h][:, g, t, :].bitcast(FP4X4), lhsT_scale=sws[h][:, g, t, :], rhs=codes[:].bitcast(FP8X4), rhs_scale=scales[:], start=(g == 0), stop=(g == 1))

        def c_add(u, t):
            h = u % 2
            if t == 0:
                y[u] = work.tile([128, 4, C], F32, name="y")
            nc.vector.scalar_tensor_tensor(out=y[u][:, t, :], in0=xs[u][:, t, :], scalar=sd[:, h, t : t + 1], in1=pa[u, t][:], op0=MULT, op1=ADD)

        def turn(u, t):
            pb = psum.tile([128, 4, 128], F32, name="pb", bufs=2)
            for q in range(4):
                nc.tensor.transpose(pb[:, q, :], y[u][:, t, q:C:4], ident[:])
            if t == 0:
                ybf[u] = work.tile([128, 512, 4], BF16, name="ybf", align_bytes=256)
            nc.scalar.copy(out=ybf[u][:, 128 * t : 128 * t + 128, :], in_=pb[:].rearrange("p q m -> p m q"))

        def f_mul(engine, u, t):
            if t == 0:
                ycd[u] = work.tile([128, 4, C], F32, name="ycd")
            engine.tensor_tensor(out=ycd[u][:, t, :], in0=y[u][:, t, :], in1=cd[:], op=MULT)

        def quant_y(u):
            yq[u] = quantize(ybf[u], "yq", 2)

        def s2(u, t):
            pc[2, u, t] = psum.tile([128, 512], F32, name="pc", bufs=3)
            codes, scales = yq[u]
            nc.tensor.matmul_mx(out=pc[2, u, t][:], lhsT=codes[:, 128 * t : 128 * t + 128].bitcast(FP8X4), lhsT_scale=scales[:, 128 * t : 128 * t + 128], rhs=bl[:].bitcast(FP4X4), rhs_scale=bls[:], start=True, stop=True)

        def z_tile(u):
            if u not in z:
                z[u] = work.tile([128, 4, C], F32, name="z", bufs=3)
            return z[u]

        def g_add(u, t):
            nc.vector.tensor_tensor(out=z_tile(u)[:, t, :], in0=pc[2, u, t][:], in1=ycd[u][:, t, :], op=ADD)

        def g_off(u, t):
            ext[u, t] = work.tile([128, C], F32, name="ext")
            nc.scalar.copy(out=ext[u, t][:], in_=pc[2, u, t][:])
            nc.gpsimd.tensor_tensor(out=z_tile(u)[:, t, :], in0=ext[u, t][:], in1=ycd[u][:, t, :], op=ADD)

        def h_round(copy, u, c0, c1):
            if u not in zbf:
                zbf[u] = work.tile([128, C, 4], BF16, name="zbf", align_bytes=256)
            copy(out=zbf[u][:, c0:c1, :].rearrange("p (c i) t -> p c t i", i=4), in_=z[u][:, :, c0:c1].rearrange("p t (c i) -> p c t i", i=4))

        def quant_z(u):
            zq[u] = quantize(zbf[u], "zq", 2)

        def s3(u, t):
            h = u % 2
            pc[3, u, t] = psum.tile([128, 512], F32, name="pc", bufs=3)
            codes, scales = zq[u]
            nc.tensor.matmul_mx(out=pc[3, u, t][:], lhsT=ac[h][:, t, :].bitcast(FP4X4), lhsT_scale=acs[h][:, t, :], rhs=codes[:].bitcast(FP8X4), rhs_scale=scales[:], start=True, stop=True)

        def j_add(u, t):
            b, h = divmod(u, 2)
            if t == 0:
                o[u] = work.tile([128, 4, C], F32, name="o")
            nc.vector.scalar_tensor_tensor(out=o[u][:, t, :], in0=z[u][:, t, :], scalar=ad[:, h, t : t + 1], in1=pc[3, u, t][:], op0=MULT, op1=ADD)
            rows = out[b, 512 * h : 512 * h + 512, :].rearrange("(p t) c -> p t c", t=4)
            if u == UNITS - 1:
                nc.sync.dma_start(out=rows[:, t, :], in_=o[u][:, t, :])
            elif t == 3:
                nc.sync.dma_start(out=rows, in_=o[u][:])

        interleave(nc.scalar.copy, 0, HEAD_V, C)
        interleave(nc.scalar.copy, 1, HEAD_V, C)
        perm_swing(0)
        interleave(nc.vector.tensor_copy, 0, 0, HEAD_V)
        perm_swing_scales(0)
        quant_x(0)
        perm_swing(1)
        interleave(nc.vector.tensor_copy, 1, 0, HEAD_V)
        quant_x(1)
        for k in (0, 2, 4, 1, 3, 5):
            s1_pass(0, k)
        interleave(nc.scalar.copy, 2, 0, C)

        for s in range(UNITS + 2):
            z_unit = s - 1 if 0 <= s - 1 < UNITS else None
            o_unit = s - 2 if 0 <= s - 2 < UNITS else None
            off = OFF[z_unit] if z_unit is not None else ()
            own = [t for t in range(4) if t not in off] if z_unit is not None else []
            fills = [(s2, z_unit, t) for t in list(off) + own]
            if o_unit is not None:
                fills += [(s3, o_unit, t) for t in range(4)]

            def fill():
                if fills:
                    fn, u, t = fills.pop(0)
                    fn(u, t)

            late = [6, 7] if s < UNITS else []
            early = list(range(6)) if s + 1 < UNITS else []

            def swing_pass():
                if early:
                    s1_pass(s + 1, early.pop(0))

            def c_pair(t0):
                for t in (t0, t0 + 1):
                    c_add(s, t)
                    if s > 0 or t < 2:
                        f_mul(nc.gpsimd, s, t)
                turn(s, t0)
                if t0 == 0:
                    for k in late:
                        s1_pass(s, k)
                else:
                    if s > 0:
                        swing_pass()
                        swing_pass()
                    if o_unit is not None:
                        j_add(o_unit, 0)
                        fill()
                turn(s, t0 + 1)

            fill()
            fill()
            fill()
            for t in off:
                g_off(z_unit, t)
                fill()
            ai = s + 3
            if ai < UNITS and s > 0:
                interleave(nc.scalar.copy, ai, 0, 256)
            if s < UNITS:
                c_pair(0)
            for n, t in enumerate(own):
                g_add(z_unit, t)
                fill()
                if n < 2:
                    swing_pass()
            if z_unit is not None:
                h_round(nc.scalar.copy, z_unit, 0, 256)
                h_round(nc.scalar.copy, z_unit, 256, 512)
            if s < UNITS:
                c_pair(2)
            if s == 0:
                perm_swing_scales(1)
                f_mul(nc.vector, 0, 2)
                f_mul(nc.vector, 0, 3)
            if o_unit is not None:
                for t in range(0 if s >= UNITS else 1, 4):
                    j_add(o_unit, t)
                    fill()
                    swing_pass()
            if s == 0:
                interleave(nc.scalar.copy, 3, 0, 256)
                interleave(nc.vector.tensor_copy, 3, 256, C)
                quant_x(2)
            elif ai < UNITS:
                interleave(nc.scalar.copy, ai, 256, C)
            while early:
                swing_pass()
            if s == 1:
                perm_accent(0)
            if s == 2:
                perm_accent(1)
            if z_unit is not None:
                quant_z(z_unit)
            if s < UNITS:
                quant_y(s)
            if ai < UNITS:
                quant_x(ai)
